import numpy as np, ml_dtypes
CORES = [96,97,98,99,100,101,102,103,112,113,114,115,116,117,118,119]
N = 16
ROOT = 12
def setup_inputs(rng):
    return {"x": rng.standard_normal((N, 128, 8), dtype=np.float32).astype(ml_dtypes.bfloat16)}
def reference(x):
    y = np.full(x.shape, np.nan, x.dtype)
    y[ROOT] = x.max(axis=0)
    return {"y": y}

from concourse.bass import DstId, RemoteDMATransfer

SCRATCH = {
    "stage": ("dram", [128, 8], "bfloat16"),
    "gat": ("dram", [16, 128, 8], "bfloat16"),
    "land": ("dram", [128, 8], "bfloat16"),
}
SEMAPHORES = ["loaded", "sent", "arrived", "res", "stored"]

FOLDER = 117


def rank_program(g, core, T, topo):
    rank = T.rank_of(core)
    if rank is None:
        return
    root = T.cores[T.root if T.root is not None else 12]

    if core == FOLDER:
        g.sync.dma_start(T.gat[rank], T.x[:]).then_inc(T.sem.arrived, 16)
        total = 16
        for c in T.cores:
            if c != core:
                total += 16 if topo.chip(c) == topo.chip(core) else 8
        g.wait_ge(T.sem.arrived, total)
        rid, pid, _s = topo.addr(root)
        g.remote_dma_fused(
            [RemoteDMATransfer(dst_ids=[DstId(rid=rid, pnc=pid)], dma_engine_mask=topo.mask(core, root),
                               remote_sem=T.sem.res, srcs=[T.gat[r] for r in range(len(T.cores))],
                               dsts=[T.land[:]], alu_op=2)],
            local_sem=T.sem.sent)
        g.wait_ge(T.sem.sent, 16)
        return

    g.sync.dma_start(T.stage[:], T.x[:]).then_inc(T.sem.loaded, 16)
    g.wait_ge(T.sem.loaded, 16)
    rid, pid, _s = topo.addr(FOLDER)
    m = topo.mask(core, FOLDER)
    g.remote_dma(T.gat[rank], T.stage[:], T.sem.arrived, T.sem.sent, pid, rid, m)

    if core == root:
        g.sync.wait_ge(T.sem.res, 16)
        g.sync.dma_start(T.y[:], T.land[:]).then_inc(T.sem.stored, 16)
        g.sync.wait_ge(T.sem.stored, 16)
    g.wait_ge(T.sem.sent, 16 if m == 0xFFFF else 8)
